import numpy as np
import ml_dtypes


def mxq(x, axis, fmt="e4m3"):
    dtype, down = {"e4m3": (ml_dtypes.float8_e4m3fn, 7), "e5m2": (ml_dtypes.float8_e5m2, 14)}[fmt]
    v = np.moveaxis(np.asarray(x, np.float32).astype(ml_dtypes.bfloat16).astype(np.float64), axis, -1)
    blocks = v.reshape(v.shape[:-1] + (-1, 32))
    amax = np.abs(blocks).max(-1, keepdims=True)
    byte = np.maximum(np.where(amax > 0, np.frexp(amax)[1] - 1 + 127, 0) - down, 1)
    scale = np.exp2(byte - 127.0)
    codes = (blocks / scale).astype(np.float32).astype(dtype).astype(np.float64)
    return np.moveaxis((codes * scale).reshape(v.shape), -1, axis)


WIDE = False


def mx_kscale(k):
    if not WIDE:
        return np.ones(k)
    levels = np.array([10, -10, 5, -5, 0])
    if k % 512:
        return np.exp2(np.random.permutation(np.resize(levels, k // 32))).repeat(32)
    a = np.empty((k // 512, 16))
    for p in range(k // 512):
        a[p, :8] = np.random.permutation(np.resize(levels, 8))
        for g in range(8):
            far = levels[np.abs(levels - a[p, g]) >= 10]
            a[p, g + 8] = far[np.random.randint(len(far))]
    return np.exp2(a.ravel()).repeat(32)


def f64(x):
    return np.asarray(x).astype(np.float64)


def striped(idx):
    return np.tile(idx.reshape(-1, 16).T, (8, 1)).astype(np.uint16)


def unstriped(offs):
    return offs[:16].T.reshape(-1).astype(np.int64)


def striped8(idx):
    return np.concatenate([x.reshape(-1, 16).T for x in idx]).astype(np.uint16)


def runs(offs, k):
    lists = np.stack([offs[16 * r : 16 * r + 16].T.reshape(-1) for r in range(8)]).astype(np.int64)
    return lists[np.arange(k) % 512 // 64]


def pack_weight(w):
    k, n = w.shape
    w = f64(np.asarray(w, np.float32).astype(ml_dtypes.bfloat16)).reshape(k // 32, 32, n)
    amax = np.abs(w).max(1)
    byte = np.clip(np.where(amax > 0, np.frexp(amax)[1] - 1 + 127 - 7, 1), 1, 254)
    scaled = (w * np.exp2(127.0 - byte)[:, None, :]).reshape(k, n).astype(np.float32)
    words = np.ascontiguousarray(scaled.reshape(k // 512, 128, 4, n).transpose(0, 1, 3, 2)).astype(ml_dtypes.float8_e4m3fn).view(np.uint8)
    return words, np.ascontiguousarray(byte.astype(np.uint8).reshape(k // 512, 16, n))


def unpack_weight(words, scales):
    g, p, n, _ = words.shape
    vals = np.ascontiguousarray(words).view(ml_dtypes.float8_e4m3fn).astype(np.float64) * np.repeat(np.exp2(scales.astype(np.float64) - 127.0), 8, axis=1)[..., None]
    return vals.transpose(0, 1, 3, 2).reshape(g * 512, n)


def sigmoid(v):
    return 1.0 / (1.0 + np.exp(-np.maximum(v, -700.0)))


K, T, S, N, H, W = 512, 2048, 512, 512, 512, 2048


def setup_inputs():
    n = np.random.standard_normal
    s = mx_kscale(K)[:, None]
    u = mx_kscale(H)
    packed_xT = pack_weight(n((K, T)) * s)
    return {
        "x_words": packed_xT[0],
        "x_scales": packed_xT[1],
        "w1": (n((K, H)) / np.sqrt(K) / s).astype(np.float32),
        "w2": (n((K, H)) / np.sqrt(K) / s).astype(np.float32),
        "gn": (np.random.uniform(0.5, 1.5, (H, 1)) * u[:, None]).astype(np.float32),
        "w3": (n((H, N)) / np.sqrt(H) / u[:, None]).astype(np.float32),
        "sl": np.random.uniform(1.5, 3.0, (N, 1)).astype(np.float32),
        "th": (0.5 * n((N, 1))).astype(np.float32),
        "offs": striped(np.random.permutation(T)[:S]),
        "two": striped(np.random.permutation(T)[:S]),
        "n1": striped8(np.stack([np.random.permutation(S) for _ in range(8)])),
        "n2": striped8(np.stack([np.random.permutation(S) for _ in range(8)])),
        "n3": striped(np.random.randint(0, S, W)),
    }


def reference(x_words, x_scales, w1, w2, gn, w3, sl, th, offs, two, n1, n2, n3):
    xq = unpack_weight(x_words, x_scales)[:, unstriped(offs)]
    y = mxq(f64(w1), 0, "e4m3").T @ xq
    x_two = unpack_weight(x_words, x_scales)[:, unstriped(two)]
    d = mxq(f64(w2), 0, "e4m3").T @ x_two
    z = f64(gn) * (y * (sigmoid(d[np.arange(H)[:, None], runs(n2, H)])) - (0.5 * (y[np.arange(H)[:, None], runs(n1, H)])))
    h = mxq(f64(w3), 0, "e4m3").T @ mxq(z, 0, "e4m3")
    sg = sigmoid(f64(sl) * (h[:, unstriped(n3)] - f64(th)))
    cnt = sg.reshape(N, S, 4).sum(axis=2)
    return np.maximum(h, cnt + -1.5)

@@ -1,0 +1,167 @@
+from contextlib import ExitStack
+
+import concourse.mybir as mybir
+
+K, T, S, N, H, W = 512, 2048, 512, 512, 512, 2048
+FLOPS = 2 * 3 * 512 * 512 * 512
+
+F32 = mybir.dt.float32
+BF16 = mybir.dt.bfloat16
+I32 = mybir.dt.int32
+U32 = mybir.dt.uint32
+U16 = mybir.dt.uint16
+U8 = mybir.dt.uint8
+FP8X4 = mybir.dt.float8_e4m3fn_x4
+ALU = mybir.AluOpType
+ACT = mybir.ActivationFunctionType
+P = 128
+HALF = 256
+
+
+def tile_picked_twlgatebegc_none_p_kernel(tc, x_words, x_scales, w1, w2, gn, w3, sl, th, offs, two, n1, n2, n3, out):
+    nc = tc.nc
+    with ExitStack() as ctx:
+        keep = ctx.enter_context(tc.tile_pool(name="keep", bufs=1))
+        ring = ctx.enter_context(tc.tile_pool(name="ring", bufs=6))
+        psum = ctx.enter_context(tc.psum_pool(name="psum", bufs=1))
+
+        def kt(shape, dt, name):
+            return keep.tile(shape, dt, name=name, align_bytes=64)
+
+        xw = kt([P, T], I32, "xw")
+        xs = kt([P, T], U8, "xs")
+        nc.vector.memset(xs[:].bitcast(I32), 0)
+        nc.sync.dma_start(xw[:], x_words[0].rearrange("p c r -> p (c r)").bitcast(I32))
+        xs_in = kt([P, T // 4], I32, "xs_in")
+        for q in range(4):
+            nc.scalar.dma_start(xs_in[32 * q : 32 * q + 4, :], x_scales[0, 4 * q : 4 * q + 4, :].bitcast(I32))
+        for q in range(4):
+            nc.vector.tensor_copy(xs[32 * q : 32 * q + 4, :].bitcast(I32), xs_in[32 * q : 32 * q + 4, :])
+        lists = {}
+        for name, src in (("two", two), ("offs", offs), ("n2", n2), ("n1", n1), ("n3", n3)):
+            lists[name] = keep.tile(list(src.shape), U16, name="list_" + name)
+        nc.sync.dma_start(lists["two"][:], two)
+        nc.sync.dma_start(lists["offs"][:], offs)
+        raw = {}
+        for name, w in (("w2", w2), ("w1", w1)):
+            for a in range(2):
+                raw[name, a] = kt([P, 4, HALF], F32, "raw_%s_%d" % (name, a))
+                nc.sync.dma_start(raw[name, a][:], w.rearrange("(p j) c -> p j c", j=4)[:, :, a * HALF : (a + 1) * HALF])
+        nc.sync.dma_start(lists["n2"][:], n2)
+        nc.sync.dma_start(lists["n1"][:], n1)
+        raw3 = kt([P, 4, N], F32, "raw3")
+        nc.sync.dma_start(raw3[:], w3.rearrange("(p j) c -> p j c", j=4))
+        nc.sync.dma_start(lists["n3"][:], n3)
+        gain = kt([P, 4], F32, "gain")
+        slope = kt([P, 4], F32, "slope")
+        thr = kt([P, 4], F32, "thr")
+        for tl, src in ((gain, gn), (slope, sl), (thr, th)):
+            nc.gpsimd.dma_start(tl[:], src.rearrange("(p t) o -> p (t o)", t=4))
+
+        def pick(name):
+            words = kt([P, S], U32, "pw_" + name)
+            scales = kt([P, S], U8, "ps_" + name)
+            nc.vector.tensor_copy(words[:], xw[:].bitcast(U32).indirect(lists[name][:]))
+            nc.vector.tensor_copy(scales[:], xs[:].indirect(lists[name][:]))
+            return words, scales
+
+        def deal(name, engines):
+            grouped = kt([P, 4, P, 4], BF16, "grouped_" + name)
+            for a in range(2):
+                dst = grouped[:, :, 64 * a : 64 * a + 64, :].rearrange("p t m j -> p m t j")
+                srcv = raw[name, a][:].rearrange("p j (m t) -> p m t j", t=4)
+                if engines[a] == "s":
+                    nc.scalar.copy(dst, srcv)
+                else:
+                    nc.vector.tensor_copy(dst, srcv)
+            return grouped
+
+        def quant(src, width, name):
+            codes = kt([P, width], U32, "codes_" + name)
+            scales = kt([P, width], U8, "scales_" + name)
+            nc.vector.quantize_mx(out=codes[:].bitcast(FP8X4), scales=scales[:], in_=src)
+            return codes, scales
+
+        def mm(dst, lhs, rhs):
+            nc.tensor.matmul_mx(out=dst, lhsT=lhs[0][:].bitcast(FP8X4), lhsT_scale=lhs[1][:], rhs=rhs[0][:].bitcast(FP8X4), rhs_scale=rhs[1][:], start=True, stop=True)
+
+        x2 = pick("two")
+        g2 = deal("w2", "ss")
+        dps = []
+        for t in range(4):
+            wq = quant(g2[:, t, :, :].rearrange("p m j -> p (m j)"), P, "w2_%d" % t)
+            bank = psum.tile([P, S], F32, name="d%d" % t, tag="bank%d" % t)
+            mm(bank[:], wq, x2)
+            dps.append(bank)
+        x1 = pick("offs")
+        g1w = deal("w1", "sv")
+        yps = []
+        for t in range(4):
+            wq = quant(g1w[:, t, :, :].rearrange("p m j -> p (m j)"), P, "w1_%d" % t)
+            bank = psum.tile([P, S], F32, name="y%d" % t, tag="bank%d" % (4 + t))
+            mm(bank[:], wq, x1)
+            yps.append(bank)
+
+        sd = []
+        for t in range(4):
+            tl = kt([P, S], F32, "sd%d" % t)
+            nc.scalar.activation(tl[:], dps[t][:], ACT.Sigmoid)
+            sd.append(tl)
+        yg = []
+        for t in range(4):
+            tl = kt([P, S], F32, "yg%d" % t)
+            if t % 2 == 0:
+                nc.vector.tensor_scalar(tl[:], yps[t][:], gain[:, t : t + 1], None, ALU.mult)
+            else:
+                nc.scalar.activation(tl[:], yps[t][:], ACT.Copy, scale=gain[:, t : t + 1])
+            yg.append(tl)
+
+        bias = kt([P, 4], F32, "bias")
+        nc.vector.scalar_tensor_tensor(bias[:], thr[:], -1.0, slope[:], ALU.mult, ALU.mult)
+
+        def w3_tile(t):
+            grouped = kt([P, P, 4], BF16, "grouped_w3_%d" % t)
+            nc.vector.tensor_copy(grouped[:], raw3[:].rearrange("p j (m t) -> p t m j", t=4)[:, t, :, :])
+            return quant(grouped[:].rearrange("p m j -> p (m j)"), P, "w3_%d" % t)
+
+        hw = [kt([P, 2 * S], F32, "hw%d" % t) for t in range(4)]
+        w3q = [w3_tile(0)]
+        zq = []
+        hps = [psum.tile([P, S], F32, name="h%d" % t, tag="bank%d" % t) for t in range(4)]
+        for a in range(2):
+            cols = slice(a * HALF, (a + 1) * HALF)
+            lcols = slice(16 * a, 16 * a + 16)
+            zb = kt([P, 4, HALF], BF16, "zb%d" % a)
+            for t in range(4):
+                nb = kt([P, HALF], F32, "nb%d_%d" % (a, t))
+                nc.scalar.activation(nb[:], yg[t][:].indirect(lists["n1"][:, lcols]), ACT.Copy)
+                prod = hw[t][:, S + a * HALF : S + (a + 1) * HALF]
+                nc.vector.tensor_tensor(prod, sd[t][:].indirect(lists["n2"][:, lcols]), yg[t][:, cols], ALU.mult)
+                nc.vector.scalar_tensor_tensor(zb[:, t, :], nb[:], -0.5, prod, ALU.mult, ALU.add)
+            zi = kt([P, HALF, 4], BF16, "zi%d" % a)
+            nc.vector.tensor_copy(zi[:], zb[:].rearrange("p t n -> p n t"))
+            zq.append(quant(zi[:].rearrange("p n t -> p (n t)"), HALF, "z%d" % a))
+            mm(hps[0][:, cols], w3q[0], zq[a])
+            nc.vector.tensor_copy(hw[0][:, cols], hps[0][:, cols])
+
+        out_v = out.rearrange("(p t) n -> p t n", t=4)
+        for t in range(4):
+            if t + 1 < 4:
+                w3q.append(w3_tile(t + 1))
+                for a in range(2):
+                    mm(hps[t + 1][:, a * HALF : (a + 1) * HALF], w3q[t + 1], zq[a])
+                nc.vector.tensor_copy(hw[t + 1][:, 0:S], hps[t + 1][:])
+            widths = [128, 128, 128, 128] if t < 3 else [128, 128, 128, 64, 64]
+            res = kt([P, S], F32, "res%d" % t)
+            c0 = 0
+            for wd in widths:
+                sg = ring.tile([P, 4 * wd], F32, name="sg")
+                nc.scalar.activation(sg[:], hw[t][:].indirect(lists["n3"][:, c0 // 4 : (c0 + wd) // 4]), ACT.Sigmoid, bias=bias[:, t : t + 1], scale=slope[:, t : t + 1])
+                cnt = ring.tile([P, wd], F32, name="cnt")
+                nc.vector.tensor_reduce(cnt[:], sg[:].rearrange("p (n f) -> p n f", f=4), mybir.AxisListType.X, ALU.add)
+                nc.vector.scalar_tensor_tensor(res[:, c0 : c0 + wd], cnt[:], -1.5, hw[t][:, c0 : c0 + wd], ALU.add, ALU.max)
+                if t == 3:
+                    nc.sync.dma_start(out_v[:, t, c0 : c0 + wd], res[:, c0 : c0 + wd])
+                c0 = c0 + wd
+            if t < 3:
+                nc.sync.dma_start(out_v[:, t, :], res[:])

@@ -25,42 +25,44 @@ def tile_picked_twlgatebegc_none_p_kernel(tc, x_words, x_scales, w1, w2, gn, w3,
         ring = ctx.enter_context(tc.tile_pool(name="ring", bufs=6))
         psum = ctx.enter_context(tc.psum_pool(name="psum", bufs=1))
 
-        def kt(shape, dt, name):
-            return keep.tile(shape, dt, name=name, align_bytes=64)
+        def kt(shape, dt, name, tag=None):
+            return keep.tile(shape, dt, name=name, tag=tag or name, align_bytes=64)
 
+        warm = kt([P, 1], F32, "warm")
+        nc.vector.memset(warm[:], 0.0)
+        nc.scalar.activation(warm[:], warm[:], ACT.Sigmoid)
         xw = kt([P, T], I32, "xw")
         xs = kt([P, T], U8, "xs")
-        nc.vector.memset(xs[:].bitcast(I32), 0)
+        nc.gpsimd.memset(xs[:].bitcast(I32), 0)
         nc.sync.dma_start(xw[:], x_words[0].rearrange("p c r -> p (c r)").bitcast(I32))
-        xs_in = kt([P, T // 4], I32, "xs_in")
-        for q in range(4):
-            nc.scalar.dma_start(xs_in[32 * q : 32 * q + 4, :], x_scales[0, 4 * q : 4 * q + 4, :].bitcast(I32))
-        for q in range(4):
-            nc.vector.tensor_copy(xs[32 * q : 32 * q + 4, :].bitcast(I32), xs_in[32 * q : 32 * q + 4, :])
         lists = {}
         for name, src in (("two", two), ("offs", offs), ("n2", n2), ("n1", n1), ("n3", n3)):
             lists[name] = keep.tile(list(src.shape), U16, name="list_" + name)
         nc.sync.dma_start(lists["two"][:], two)
+        for q in range(4):
+            nc.sync.dma_start(xs[32 * q : 32 * q + 4, :].bitcast(I32), x_scales[0, 4 * q : 4 * q + 4, :].bitcast(I32))
         nc.sync.dma_start(lists["offs"][:], offs)
         raw = {}
         for name, w in (("w2", w2), ("w1", w1)):
             for a in range(2):
                 raw[name, a] = kt([P, 4, HALF], F32, "raw_%s_%d" % (name, a))
                 nc.sync.dma_start(raw[name, a][:], w.rearrange("(p j) c -> p j c", j=4)[:, :, a * HALF : (a + 1) * HALF])
+        gain = kt([P, 4], F32, "gain")
+        slope = kt([P, 4], F32, "slope")
+        thr = kt([P, 4], F32, "thr")
+        nc.sync.dma_start(gain[:], gn.rearrange("(p t) o -> p (t o)", t=4))
         nc.sync.dma_start(lists["n2"][:], n2)
         nc.sync.dma_start(lists["n1"][:], n1)
         raw3 = kt([P, 4, N], F32, "raw3")
         nc.sync.dma_start(raw3[:], w3.rearrange("(p j) c -> p j c", j=4))
         nc.sync.dma_start(lists["n3"][:], n3)
-        gain = kt([P, 4], F32, "gain")
-        slope = kt([P, 4], F32, "slope")
-        thr = kt([P, 4], F32, "thr")
-        for tl, src in ((gain, gn), (slope, sl), (thr, th)):
-            nc.gpsimd.dma_start(tl[:], src.rearrange("(p t) o -> p (t o)", t=4))
+        with nc.allow_non_contiguous_dma(reason="one value a row"):
+            for tl, src in ((slope, sl), (thr, th)):
+                nc.sync.dma_start(tl[:], src.rearrange("(t p) o -> p (t o)", t=4))
 
-        def pick(name):
+        def pick(name, tag=None):
             words = kt([P, S], U32, "pw_" + name)
-            scales = kt([P, S], U8, "ps_" + name)
+            scales = kt([P, S], U8, "ps_" + name, tag)
             nc.vector.tensor_copy(words[:], xw[:].bitcast(U32).indirect(lists[name][:]))
             nc.vector.tensor_copy(scales[:], xs[:].indirect(lists[name][:]))
             return words, scales
@@ -93,7 +95,7 @@ def tile_picked_twlgatebegc_none_p_kernel(tc, x_words, x_scales, w1, w2, gn, w3,
             bank = psum.tile([P, S], F32, name="d%d" % t, tag="bank%d" % t)
             mm(bank[:], wq, x2)
             dps.append(bank)
-        x1 = pick("offs")
+        x1 = pick("offs", "grouped_w2")
         g1w = deal("w1", "sv")
         yps = []
         for t in range(4):
@@ -110,48 +112,77 @@ def tile_picked_twlgatebegc_none_p_kernel(tc, x_words, x_scales, w1, w2, gn, w3,
         yg = []
         for t in range(4):
             tl = kt([P, S], F32, "yg%d" % t)
-            if t % 2 == 0:
-                nc.vector.tensor_scalar(tl[:], yps[t][:], gain[:, t : t + 1], None, ALU.mult)
-            else:
-                nc.scalar.activation(tl[:], yps[t][:], ACT.Copy, scale=gain[:, t : t + 1])
             yg.append(tl)
 
         bias = kt([P, 4], F32, "bias")
         nc.vector.scalar_tensor_tensor(bias[:], thr[:], -1.0, slope[:], ALU.mult, ALU.mult)
 
         def w3_tile(t):
-            grouped = kt([P, P, 4], BF16, "grouped_w3_%d" % t)
-            nc.vector.tensor_copy(grouped[:], raw3[:].rearrange("p j (m t) -> p t m j", t=4)[:, t, :, :])
+            grouped = kt([P, P, 4], BF16, "grouped_w3_%d" % t, "zi1" if t else None)
+            nc.vector.tensor_copy(grouped[:], raw3[:, :, t * P : (t + 1) * P].rearrange("p j m -> p m j"))
             return quant(grouped[:].rearrange("p m j -> p (m j)"), P, "w3_%d" % t)
 
-        hw = [kt([P, 2 * S], F32, "hw%d" % t) for t in range(4)]
+        hw = [kt([P, (4 if t < 3 else 2) * S], F32, "hw%d" % t) for t in range(4)]
         w3q = [w3_tile(0)]
-        zq = []
-        hps = [psum.tile([P, S], F32, name="h%d" % t, tag="bank%d" % t) for t in range(4)]
-        for a in range(2):
+        zq = {}
+        zb = [kt([P, 4, HALF], BF16, "zb%d" % a) for a in range(2)]
+        zi = [kt([P, HALF, 4], BF16, "zi0"), kt([P, P, 4], BF16, "zi1"), kt([P, P, 4], BF16, "zi2")]
+        pieces = [(0, HALF), (HALF, P), (HALF + P, P)]
+
+        def weave(eng, i):
+            c0, wd = pieces[i]
+            a, n0 = divmod(c0, HALF)
+            eng(zi[i][:], zb[a][:, :, n0 : n0 + wd].rearrange("p t n -> p n t"))
+
+        def second(i):
+            c0, wd = pieces[i]
+            zq[i] = (quant(zi[i][:].rearrange("p n t -> p (n t)"), wd, "z%d" % i))
+            mm(h0[i][:, 0:wd], w3q[0], zq[i])
+
+        def prod_of(a, t):
+            return hw[t][:, S + a * HALF : S + (a + 1) * HALF]
+
+        def gated(a, t):
             cols = slice(a * HALF, (a + 1) * HALF)
             lcols = slice(16 * a, 16 * a + 16)
-            zb = kt([P, 4, HALF], BF16, "zb%d" % a)
-            for t in range(4):
-                nb = kt([P, HALF], F32, "nb%d_%d" % (a, t))
-                nc.scalar.activation(nb[:], yg[t][:].indirect(lists["n1"][:, lcols]), ACT.Copy)
-                prod = hw[t][:, S + a * HALF : S + (a + 1) * HALF]
-                nc.vector.tensor_tensor(prod, sd[t][:].indirect(lists["n2"][:, lcols]), yg[t][:, cols], ALU.mult)
-                nc.vector.scalar_tensor_tensor(zb[:, t, :], nb[:], -0.5, prod, ALU.mult, ALU.add)
-            zi = kt([P, HALF, 4], BF16, "zi%d" % a)
-            nc.vector.tensor_copy(zi[:], zb[:].rearrange("p t n -> p n t"))
-            zq.append(quant(zi[:].rearrange("p n t -> p (n t)"), HALF, "z%d" % a))
-            mm(hps[0][:, cols], w3q[0], zq[a])
-            nc.vector.tensor_copy(hw[0][:, cols], hps[0][:, cols])
+            if a == 0 and t == 0:
+                nc.vector.tensor_scalar(yg[t][:], yps[t][:], gain[:, t : t + 1], None, ALU.mult)
+            elif a == 0:
+                nc.scalar.activation(yg[t][:], yps[t][:], ACT.Copy, scale=gain[:, t : t + 1])
+            nc.vector.tensor_tensor(prod_of(a, t), sd[t][:].indirect(lists["n2"][:, lcols]), yg[t][:, cols], ALU.mult)
 
-        out_v = out.rearrange("(p t) n -> p t n", t=4)
+        def combine(a, t):
+            nb = kt([P, HALF], F32, "nb%d_%d" % (a, t))
+            nc.scalar.activation(nb[:], yg[t][:].indirect(lists["n1"][:, 16 * a : 16 * a + 16]), ACT.Copy)
+            cuts = (0, P, HALF) if (a, t) == (1, 3) else (0, HALF)
+            for lo, hi in zip(cuts, cuts[1:]):
+                nc.vector.scalar_tensor_tensor(zb[a][:, t, lo:hi], nb[:, lo:hi], -0.5, prod_of(a, t)[:, lo:hi], ALU.mult, ALU.add)
+
+        h0 = [psum.tile([P, S], F32, name="h0_%d" % i, tag="bank%d" % (4 + i)) for i in range(3)]
+        steps = [(a, t) for a in range(2) for t in range(4)]
+        gated(*steps[0])
+        for i in range(8):
+            if i + 1 < 8:
+                gated(*steps[i + 1])
+            combine(*steps[i])
+        weave(nc.scalar.copy, 0)
+        weave(nc.vector.tensor_copy, 1)
+        weave(nc.vector.tensor_copy, 2)
+        for i in (1, 2, 0):
+            second(i)
+        for i in (1, 2, 0):
+            c0, wd = pieces[i]
+            nc.scalar.copy(hw[0][:, c0 : c0 + wd], h0[i][:, 0:wd])
+        for t in range(1, 4):
+            w3q.append(w3_tile(t))
+            bank = psum.tile([P, S], F32, name="h%d" % t, tag="bank%d" % t)
+            for i, (c0, wd) in enumerate(pieces):
+                mm(bank[:, c0 : c0 + wd], w3q[t], zq[i])
+            nc.vector.tensor_copy(hw[t][:, 0:S], bank[:])
+
+        out_v = out.rearrange("(t p) n -> p t n", t=4)
         for t in range(4):
-            if t + 1 < 4:
-                w3q.append(w3_tile(t + 1))
-                for a in range(2):
-                    mm(hps[t + 1][:, a * HALF : (a + 1) * HALF], w3q[t + 1], zq[a])
-                nc.vector.tensor_copy(hw[t + 1][:, 0:S], hps[t + 1][:])
-            widths = [128, 128, 128, 128] if t < 3 else [128, 128, 128, 64, 64]
+            widths = [256, 256] if t < 3 else [128, 128, 128, 64, 64]
             res = kt([P, S], F32, "res%d" % t)
             c0 = 0
             for wd in widths:

from contextlib import ExitStack

import concourse.mybir as mybir

K, T, S, N, H, W = 512, 2048, 512, 512, 512, 2048
FLOPS = 2 * 3 * 512 * 512 * 512

F32 = mybir.dt.float32
BF16 = mybir.dt.bfloat16
I32 = mybir.dt.int32
U32 = mybir.dt.uint32
U16 = mybir.dt.uint16
U8 = mybir.dt.uint8
FP8X4 = mybir.dt.float8_e4m3fn_x4
ALU = mybir.AluOpType
ACT = mybir.ActivationFunctionType
P = 128
HALF = 256


def tile_picked_twlgatebegc_none_p_kernel(tc, x_words, x_scales, w1, w2, gn, w3, sl, th, offs, two, n1, n2, n3, out):
    nc = tc.nc
    with ExitStack() as ctx:
        keep = ctx.enter_context(tc.tile_pool(name="keep", bufs=1))
        ring = ctx.enter_context(tc.tile_pool(name="ring", bufs=6))
        psum = ctx.enter_context(tc.psum_pool(name="psum", bufs=1))

        def kt(shape, dt, name, tag=None):
            return keep.tile(shape, dt, name=name, tag=tag or name, align_bytes=64)

        warm = kt([P, 1], F32, "warm")
        nc.vector.memset(warm[:], 0.0)
        nc.scalar.activation(warm[:], warm[:], ACT.Sigmoid)
        xw = kt([P, T], I32, "xw")
        xs = kt([P, T], U8, "xs")
        nc.gpsimd.memset(xs[:].bitcast(I32), 0)
        nc.sync.dma_start(xw[:], x_words[0].rearrange("p c r -> p (c r)").bitcast(I32))
        lists = {}
        for name, src in (("two", two), ("offs", offs), ("n2", n2), ("n1", n1), ("n3", n3)):
            lists[name] = keep.tile(list(src.shape), U16, name="list_" + name)
        nc.sync.dma_start(lists["two"][:], two)
        for q in range(4):
            nc.sync.dma_start(xs[32 * q : 32 * q + 4, :].bitcast(I32), x_scales[0, 4 * q : 4 * q + 4, :].bitcast(I32))
        nc.sync.dma_start(lists["offs"][:], offs)
        raw = {}
        for name, w in (("w2", w2), ("w1", w1)):
            for a in range(2):
                raw[name, a] = kt([P, 4, HALF], F32, "raw_%s_%d" % (name, a))
                nc.sync.dma_start(raw[name, a][:], w.rearrange("(p j) c -> p j c", j=4)[:, :, a * HALF : (a + 1) * HALF])
        gain = kt([P, 4], F32, "gain")
        slope = kt([P, 4], F32, "slope")
        thr = kt([P, 4], F32, "thr")
        nc.sync.dma_start(gain[:], gn.rearrange("(p t) o -> p (t o)", t=4))
        nc.sync.dma_start(lists["n2"][:], n2)
        nc.sync.dma_start(lists["n1"][:], n1)
        raw3 = kt([P, 4, N], F32, "raw3")
        nc.sync.dma_start(raw3[:], w3.rearrange("(p j) c -> p j c", j=4))
        nc.sync.dma_start(lists["n3"][:], n3)
        with nc.allow_non_contiguous_dma(reason="one value a row"):
            for tl, src in ((slope, sl), (thr, th)):
                nc.sync.dma_start(tl[:], src.rearrange("(t p) o -> p (t o)", t=4))

        def pick(name, tag=None):
            words = kt([P, S], U32, "pw_" + name)
            scales = kt([P, S], U8, "ps_" + name, tag)
            nc.vector.tensor_copy(words[:], xw[:].bitcast(U32).indirect(lists[name][:]))
            nc.vector.tensor_copy(scales[:], xs[:].indirect(lists[name][:]))
            return words, scales

        def deal(name, engines):
            grouped = kt([P, 4, P, 4], BF16, "grouped_" + name)
            for a in range(2):
                dst = grouped[:, :, 64 * a : 64 * a + 64, :].rearrange("p t m j -> p m t j")
                srcv = raw[name, a][:].rearrange("p j (m t) -> p m t j", t=4)
                if engines[a] == "s":
                    nc.scalar.copy(dst, srcv)
                else:
                    nc.vector.tensor_copy(dst, srcv)
            return grouped

        def quant(src, width, name):
            codes = kt([P, width], U32, "codes_" + name)
            scales = kt([P, width], U8, "scales_" + name)
            nc.vector.quantize_mx(out=codes[:].bitcast(FP8X4), scales=scales[:], in_=src)
            return codes, scales

        def mm(dst, lhs, rhs):
            nc.tensor.matmul_mx(out=dst, lhsT=lhs[0][:].bitcast(FP8X4), lhsT_scale=lhs[1][:], rhs=rhs[0][:].bitcast(FP8X4), rhs_scale=rhs[1][:], start=True, stop=True)

        x2 = pick("two")
        g2 = deal("w2", "ss")
        dps = []
        for t in range(4):
            wq = quant(g2[:, t, :, :].rearrange("p m j -> p (m j)"), P, "w2_%d" % t)
            bank = psum.tile([P, S], F32, name="d%d" % t, tag="bank%d" % t)
            mm(bank[:], wq, x2)
            dps.append(bank)
        x1 = pick("offs", "grouped_w2")
        g1w = deal("w1", "sv")
        yps = []
        for t in range(4):
            wq = quant(g1w[:, t, :, :].rearrange("p m j -> p (m j)"), P, "w1_%d" % t)
            bank = psum.tile([P, S], F32, name="y%d" % t, tag="bank%d" % (4 + t))
            mm(bank[:], wq, x1)
            yps.append(bank)

        sd = []
        for t in range(4):
            tl = kt([P, S], F32, "sd%d" % t)
            nc.scalar.activation(tl[:], dps[t][:], ACT.Sigmoid)
            sd.append(tl)
        yg = []
        for t in range(4):
            tl = kt([P, S], F32, "yg%d" % t)
            yg.append(tl)

        bias = kt([P, 4], F32, "bias")
        nc.vector.scalar_tensor_tensor(bias[:], thr[:], -1.0, slope[:], ALU.mult, ALU.mult)

        def w3_tile(t):
            grouped = kt([P, P, 4], BF16, "grouped_w3_%d" % t, "zi1" if t else None)
            nc.vector.tensor_copy(grouped[:], raw3[:, :, t * P : (t + 1) * P].rearrange("p j m -> p m j"))
            return quant(grouped[:].rearrange("p m j -> p (m j)"), P, "w3_%d" % t)

        hw = [kt([P, (4 if t < 3 else 2) * S], F32, "hw%d" % t) for t in range(4)]
        w3q = [w3_tile(0)]
        zq = {}
        zb = [kt([P, 4, HALF], BF16, "zb%d" % a) for a in range(2)]
        zi = [kt([P, HALF, 4], BF16, "zi0"), kt([P, P, 4], BF16, "zi1"), kt([P, P, 4], BF16, "zi2")]
        pieces = [(0, HALF), (HALF, P), (HALF + P, P)]

        def weave(eng, i):
            c0, wd = pieces[i]
            a, n0 = divmod(c0, HALF)
            eng(zi[i][:], zb[a][:, :, n0 : n0 + wd].rearrange("p t n -> p n t"))

        def second(i):
            c0, wd = pieces[i]
            zq[i] = (quant(zi[i][:].rearrange("p n t -> p (n t)"), wd, "z%d" % i))
            mm(h0[i][:, 0:wd], w3q[0], zq[i])

        def prod_of(a, t):
            return hw[t][:, S + a * HALF : S + (a + 1) * HALF]

        def gated(a, t):
            cols = slice(a * HALF, (a + 1) * HALF)
            lcols = slice(16 * a, 16 * a + 16)
            if a == 0 and t == 0:
                nc.vector.tensor_scalar(yg[t][:], yps[t][:], gain[:, t : t + 1], None, ALU.mult)
            elif a == 0:
                nc.scalar.activation(yg[t][:], yps[t][:], ACT.Copy, scale=gain[:, t : t + 1])
            nc.vector.tensor_tensor(prod_of(a, t), sd[t][:].indirect(lists["n2"][:, lcols]), yg[t][:, cols], ALU.mult)

        def combine(a, t):
            nb = kt([P, HALF], F32, "nb%d_%d" % (a, t))
            nc.scalar.activation(nb[:], yg[t][:].indirect(lists["n1"][:, 16 * a : 16 * a + 16]), ACT.Copy)
            cuts = (0, P, HALF) if (a, t) == (1, 3) else (0, HALF)
            for lo, hi in zip(cuts, cuts[1:]):
                nc.vector.scalar_tensor_tensor(zb[a][:, t, lo:hi], nb[:, lo:hi], -0.5, prod_of(a, t)[:, lo:hi], ALU.mult, ALU.add)

        h0 = [psum.tile([P, S], F32, name="h0_%d" % i, tag="bank%d" % (4 + i)) for i in range(3)]
        steps = [(a, t) for a in range(2) for t in range(4)]
        gated(*steps[0])
        for i in range(8):
            if i + 1 < 8:
                gated(*steps[i + 1])
            combine(*steps[i])
        weave(nc.scalar.copy, 0)
        weave(nc.vector.tensor_copy, 1)
        weave(nc.vector.tensor_copy, 2)
        for i in (1, 2, 0):
            second(i)
        for i in (1, 2, 0):
            c0, wd = pieces[i]
            nc.scalar.copy(hw[0][:, c0 : c0 + wd], h0[i][:, 0:wd])
        for t in range(1, 4):
            w3q.append(w3_tile(t))
            bank = psum.tile([P, S], F32, name="h%d" % t, tag="bank%d" % t)
            for i, (c0, wd) in enumerate(pieces):
                mm(bank[:, c0 : c0 + wd], w3q[t], zq[i])
            nc.vector.tensor_copy(hw[t][:, 0:S], bank[:])

        out_v = out.rearrange("(t p) n -> p t n", t=4)
        for t in range(4):
            widths = [256, 256] if t < 3 else [128, 128, 128, 64, 64]
            res = kt([P, S], F32, "res%d" % t)
            c0 = 0
            for wd in widths:
                sg = ring.tile([P, 4 * wd], F32, name="sg")
                nc.scalar.activation(sg[:], hw[t][:].indirect(lists["n3"][:, c0 // 4 : (c0 + wd) // 4]), ACT.Sigmoid, bias=bias[:, t : t + 1], scale=slope[:, t : t + 1])
                cnt = ring.tile([P, wd], F32, name="cnt")
                nc.vector.tensor_reduce(cnt[:], sg[:].rearrange("p (n f) -> p n f", f=4), mybir.AxisListType.X, ALU.add)
                nc.vector.scalar_tensor_tensor(res[:, c0 : c0 + wd], cnt[:], -1.5, hw[t][:, c0 : c0 + wd], ALU.add, ALU.max)
                if t == 3:
                    nc.sync.dma_start(out_v[:, t, c0 : c0 + wd], res[:, c0 : c0 + wd])
                c0 = c0 + wd
            if t < 3:
                nc.sync.dma_start(out_v[:, t, :], res[:])
